import numpy as np, ml_dtypes
CORES = [10,34,74,98]
N = 4
BF = ml_dtypes.bfloat16
def gentries(a):
    return np.ascontiguousarray(a.reshape(8, 16, -1).transpose(0, 2, 1)).reshape(8, -1)
def gtable(e):
    e = np.asarray(e); return np.ascontiguousarray(e.reshape(8, -1, 16).transpose(0, 2, 1)).reshape(128, -1).astype(np.int32)
V, P, T, TL, Q, M = 3584, 256, 8, 4, 9, 4096
def money(rng, base):
    v = base + rng.integers(-3, 4, base.shape[:2] + (16, base.shape[-1]))
    return np.clip(np.floor(v), 0, 15).astype(np.int64)
def parts(rng):
    x = money(rng, 16 * rng.random((N, 8, 1, V)) ** rng.choice(np.array([2.0, 3.0, 5.0]), (N, 8, 1, 1)))
    price = money(rng, 16 * rng.random((N, 8, 1, P)))
    pool = rng.integers(0, V, (N, 8, 64))
    pop = np.take_along_axis(pool, rng.integers(0, 64, (N, 8, 16 * V)), 2).reshape(N, 8, 16, V)
    kin = np.where(rng.random((N, 8, 16, V)) < 0.15, pop, rng.integers(0, V, (N, 8, 16, V)))
    few = np.take_along_axis(pool, rng.integers(0, 48, (N, 8, P)), 2)
    own = np.where(rng.random((N, 8, P)) < 0.5, few, rng.integers(0, V, (N, 8, P)))
    hold = rng.integers(0, V, (N, 8, P)); wall = rng.integers(0, 2, (N, 8, P)); wt = rng.integers(0, 256, (N, 8, 16))
    return x, kin, own, hold, wall, price, wt
def pack(x, kin, own, hold, wall, price, wt):
    return {"x": np.ascontiguousarray(x.reshape(N, 128, V)).astype(np.float32).astype(BF), "kin": np.ascontiguousarray(kin.reshape(N, 128, V)).astype(np.int32),
            "own": np.stack([gtable(a) for a in own]), "hold": np.stack([gtable(a) for a in hold]), "wall": np.stack([gtable(a) for a in wall]),
            "price": np.ascontiguousarray(price.reshape(N, 128, P)).astype(np.float32).astype(BF), "wt": np.ascontiguousarray(wt.reshape(N, 128, 1)).astype(np.int32)}
def setup_inputs(rng):
    return pack(*parts(rng))
def setup_inputs_alike(rng):
    x, kin, own, hold, wall, price, wt = parts(rng)
    kin[:, 0] = kin[:, 0, :, :1].copy()
    kin[:, 1] = kin[:, 1, :1, :].copy()
    own[:, 2] = own[:, 2, :1].copy()
    kin[:, 3] = rng.integers(0, V, (N, 1, 1))
    own[:, 4] = np.take_along_axis(rng.integers(0, V, (N, 3)), rng.integers(0, 3, (N, P)), 1)
    own[:, 5] = np.argsort(rng.random((N, V)), axis=-1)[:, :P]; price[:, 5] = 15; x[:, 5] = 0; x[:, 5, 3] = rng.integers(0, 2, (N, V))
    own[1::2, 5, P - 1] = own[1::2, 5, 0]; price[1::2, 5, 3, P - 1] = 0
    x[:, 6] = x[:, 6, :, :1].copy(); hold[:, 6] = hold[:, 6, :1].copy()
    kin[:, 7] = rng.choice(np.array([0, 1, V - 2, V - 1]), (N, 16, V)); own[:, 7] = rng.choice(np.array([0, V - 1]), (N, P))
    return pack(x, kin, own, hold, wall, price, wt)
def setup_inputs_corners(rng):
    x, kin, own, hold, wall, price, wt = parts(rng); q = rng.permutation(8); a = np.arange(V)
    for r in range(N):
        g = q[0]; x[r, g] = 0; price[r, g] = 15; kin[r, g] = np.minimum(a + 1, V - 1); own[r, g, ::8] = V - 1; own[r, g, 1::8] = 0; own[r, g, 2::8] = V - 2
        g = q[1]; kin[r, g] = a; own[r, g, :2] = 0; own[r, g, P - 2:] = V - 1
        g = q[2]; price[r, g] = 0; wt[r, g] = 255 * (r % 2)
        g = q[3]; x[r, g] = 15; price[r, g] = 15; wt[r, g] = 255; wall[r, g] = 1; hold[r, g, ::2] = V - 1; hold[r, g, 1::4] = 0
        kin[r, g, 0] = rng.permutation(V); own[r, g] = rng.permutation(V)[:P]
        if r % 2 == 1: own[r, g, P - 1] = own[r, g, 0]; price[r, g, :, P - 1] = 7
        g = q[4 + r % 4]; kin[r, g] = rng.integers(0, 2, (16, V)) * (V - 1); own[r, g] = rng.integers(0, 2, P) * (V - 1)
        g = q[4 + (r + 1) % 4]; wall[r, g] = 0; wt[r, g] = 0
        g = q[4 + (r + 2) % 4]; x[r, g] = 0; x[r, g, :, 0] = 15; price[r, g] = 15; kin[r, g] = np.maximum(a - 1, 0); own[r, g] = rng.integers(0, 2 * T, P)
        g = q[4 + (r + 3) % 4]; wall[r, g] = 1; hold[r, g] = rng.integers(0, 2, P) * (V - 1); kin[r, g, :, V - 1] = 0; kin[r, g, :, 0] = V - 1
    return pack(x, kin, own, hold, wall, price, wt)
def setup_inputs_ends(rng):
    def rec(n):
        k = rng.random((N, 8, 1, n)); el = rng.integers(0, 2, (N, 8, 16, n))
        return 15 * np.where(k < 0.35, 0, np.where(k < 0.7, 1, el))
    x = rec(V); price = rec(P)
    kin = np.where(rng.random((N, 8, 1, V)) < 0.7, rng.integers(0, 2, (N, 8, 16, V)) * (V - 1), rng.integers(0, V, (N, 8, 16, V)))
    own = np.where(rng.random((N, 8, P)) < 0.7, rng.integers(0, 2, (N, 8, P)) * (V - 1), rng.integers(0, V, (N, 8, P)))
    hold = np.where(rng.random((N, 8, P)) < 0.75, rng.integers(0, 2, (N, 8, P)) * (V - 1), rng.integers(0, V, (N, 8, P)))
    wall = rng.integers(0, 2, (N, 8, P)); wt = 255 * rng.integers(0, 2, (N, 8, 16)); wt[N - 1, 7] = 255; wt[N - 1, 0, 0] = 0
    for g in range(8):
        x[:, g, :, 0] = (0, 15, 0, 15)[g % 4]; x[:, g, :, V - 1] = (15, 0, 0, 15)[g % 4]
    x[:, 7, :, 0] = 0; x[:, 7, :, 4] = 0; x[:, 7, :, V - 1] = 15
    kin[:, 7, :, V - 1] = V - 1; kin[:, 7, :, 0] = 0; kin[:, 7, 0::2, 2] = 4; kin[:, 7, 1::2, 2] = 0
    own[:, 7, 0] = V - 1; price[:, 7, :, 0] = 0; wall[:, 7, 0] = 0
    own[:, 7, P - 8:] = V - 1; hold[:, 7, P - 8:] = V - 1; wall[:, 7, P - 8:] = 1
    own[:, 7, P - 16:P - 8] = 0; own[:, 7, P - 24:P - 16] = 2; price[:, 7, :, P - 24:] = 15
    x[:, 5, :, V - 2] = 0; kin[:, 5, :, V - 2] = V - 2; own[:, 5, P - 2:] = V - 2; wall[:, 5, P - 2:] = 0; price[:, 5, :, P - 2:] = 15
    y = 15 >> (T // TL); s = [a for a in range(V, 61201, M) if a % y == 0][0] // y
    for r in range(N):
        wt[r, 5] = rng.permutation(np.array([255] * (s // 255) + [s % 255] + [0] * (15 - s // 255)))
    return pack(x, kin, own, hold, wall, price, wt)
def setup_inputs_spread(rng):
    def skew(top, p, *shape):
        return np.minimum(np.floor(top * rng.random(shape) ** p), top - 1).astype(np.int64)
    x = skew(16, np.exp2(rng.integers(-2, 4, (N, 8, 1, V)) + rng.integers(0, 2, (N, 8, 16, 1))), N, 8, 16, V)
    price = skew(16, np.exp2(rng.integers(-3, 3, (N, 8, 1, P)) + rng.integers(0, 2, (N, 8, 16, 1))), N, 8, 16, P)
    kin = skew(V, np.exp2(rng.integers(-1, 4, (N, 8, 16, 1))), N, 8, 16, V)
    own = skew(V, np.exp2(rng.integers(-2, 4, (N, 8, 1))), N, 8, P); hold = skew(V, np.exp2(rng.integers(-3, 4, (N, 8, 1))), N, 8, P)
    wall = (rng.random((N, 8, P)) < rng.choice(np.array([0.1, 0.5, 0.9]), (N, 8, 1))).astype(np.int64)
    wt = np.minimum(np.floor(np.exp2(8.02 * rng.random((N, 8, 16)))).astype(np.int64) - 1, 255)
    return pack(x, kin, own, hold, wall, price, wt)
def setup_inputs_ties(rng):
    x, kin, own, hold, wall, price, wt = parts(rng)
    n = Q - 2 + rng.integers(0, 2, (N, 8, 1, V)) + (rng.random((N, 8, 1, V)) < 0.03) + (np.arange(8) % 2).reshape(1, 8, 1, 1)
    x = 6 + (np.argsort(rng.random((N, 8, 16, V)), axis=2) < n).astype(np.int64)
    price = np.broadcast_to(rng.choice(np.array([6, 7, 7, 7, 7, 7, 7, 8]), (N, 8, 1, P)), (N, 8, 16, P)).copy()
    i = int(rng.integers(0, 16)); x[:, 6, :, V - 1] = 11; x[:, 6, i, V - 1] = 1
    k6 = kin[:, 6]; k6[k6 == V - 1] = V - 2; kin[:, 6, :, V - 1] = V - 1
    o6 = own[:, 6]; o6[o6 == V - 1] = 0; own[:, 6, P - 2:] = V - 1; wall[:, 6] = 0; price[:, 6, :, P - 2:] = 15
    ya, yz = 15, 15
    for _ in range(T // TL):
        ya, yz = (ya + 11) >> 1, (yz + 1) >> 1
    for r in range(N):
        s = 32768 if r % 2 == 0 else 7 * M
        c = [a for a in range(256) if (s - yz * a) % ya == 0][0]; rest = (s - yz * c) // ya
        wt[r, 6] = np.insert(rng.permutation(np.array([255] * (rest // 255) + [rest % 255] + [0] * (14 - rest // 255))), i, c)
    return pack(x, kin, own, hold, wall, price, wt)
def check_inputs(d):
    bad = []
    for k, hi in (("x", 15), ("kin", V - 1), ("own", V - 1), ("hold", V - 1), ("wall", 1), ("price", 15), ("wt", 255)):
        a = np.asarray(d[k]).astype(np.float64)
        if not (np.min(a) >= 0 and np.max(a) <= hi): bad.append("range of " + k)
        elif np.any(a != np.floor(a)): bad.append("whole numbers in " + k)
    return bad
def reference(x, kin, own, hold, wall, price, wt):
    X = x.astype(np.float32).astype(np.int32).reshape(N, 8, 16, V); K = kin.astype(np.int64).reshape(N, 8, 16, V)
    heir = np.tile(np.arange(V), (N, 8, 1)); lane = np.arange(P)
    e = np.stack([gentries(a) for a in own]).astype(np.int64); h = np.stack([gentries(a) for a in hold]).astype(np.int64); wl = np.stack([gentries(a) for a in wall])
    y = price.astype(np.float32).astype(np.int32).reshape(N, 8, 16, P); w = wt.astype(np.int64).reshape(N, 8, 16, 1)
    for t in range(T):
        for r in range(N):
            s = (r + t) % N; XS, KS, HS, ys, hs, es = X[s], K[s], heir[s], y[r], h[r], e[r].copy()
            c = np.take_along_axis(KS, es[:, None, :], 2)
            d = np.take_along_axis(XS, c.reshape(8, 1, 16 * P), 2).reshape(8, 16, 16, P) - ys[:, :, None, :]
            solvent = np.add.reduce((d >= 0).astype(np.int32), axis=1) >= Q; score = np.add.reduce(np.abs(d), axis=1)
            offers = np.any(solvent, axis=1)
            k = np.where(offers, np.argmax(solvent, axis=1), np.argmin(score, axis=1))
            b = np.take_along_axis(c, k[:, None, :], 1)[:, 0]
            key = np.where(offers, b, V + es)
            first = np.argmax(key[:, :, None] == key[:, None, :], axis=2) == lane
            fg, fp = np.nonzero(first & ~offers); ef, f = es[fg, fp], b[fg, fp]
            KS[fg, 1::2, ef] = KS[fg, 1::2, f]
            HS[fg, ef] = f
            wg, wp = np.nonzero(first & offers); cw = b[wg, wp]
            XS[wg, :, cw] = np.maximum(XS[wg, :, cw] - (ys[wg, :, wp] >> 2), 0)
            ys[wg, :, wp] = np.minimum(ys[wg, :, wp] + 1, 15); hs[wg, wp] = cw
            es = np.take_along_axis(HS, es, 1)
            if t % TL == TL - 1:
                es = np.where(wl[r] == 1, hs, es)
                y[r] = (ys + np.take_along_axis(XS, es[:, None, :], 2)) >> 1
                u = np.add.reduce(w[s] * y[r], axis=1) & (M - 1)
                h[r] = np.where(u >= V, u - V, u)
            e[r] = es
    yk = np.add.reduce(K * np.arange(1, 17).reshape(1, 1, 16, 1), axis=2)
    return {"yx": X.reshape(N, 128, V).astype(np.float32).astype(BF), "yk": yk.astype(np.float32), "yh": heir.astype(np.float32), "yo": e.astype(np.float32), "yt": h.astype(np.float32)}

@@ -1,0 +1,514 @@
+from concourse.bass import DstId, RemoteDMATransfer
+from concourse.mybir import dt, AluOpType, AxisListType, ActivationFunctionType
+
+V, NP, NT, TERM = 3584, 256, 8, 4
+W = V + NP
+CH = 64
+NCH = NP // CH
+RDF = True
+NE = 11
+BIG = float(2 ** 28)
+
+_S = {}
+
+
+def _sb(n, w, d):
+    _S[n] = ("sbuf", [128, w], d)
+
+
+F, B, I, U = "float32", "bfloat16", "int32", "uint16"
+for _n, _w, _d in [
+        ("K", W, F), ("KI", V, I), ("X", W, B), ("H", W, F), ("YK", W, F),
+        ("OWN", 16, I), ("WL", 16, I), ("WR", 16, I), ("HI0", 16, I), ("WTI", 1, I),
+        ("RE", 16 * NT, U), ("RP", NP * NT, B), ("RH", 16 * NT, F), ("FIN", 32, F),
+        ("EN", 16 * NT, U), ("PO", NP * NT, B), ("HO", 16 * NT, F), ("FO", 32, F),
+        ("CU", NP, U), ("KC0", NP, F), ("PR", 16 * NP, B), ("D", 16 * NP, B), ("AB", 16 * NP, B), ("GE", 16 * NP, B),
+        ("KB", NP, F), ("KEY", NP, F), ("T1", NP, F), ("SC", NP, F),
+        ("MI", 16, I), ("BI", 16, I), ("FB", 16, F), ("OFF", 16, F), ("KT", 16, F), ("KL", 16, F), ("EV", 16, F),
+        ("EF", 16, F), ("EMT", 16, F), ("BMT", 16, F), ("WW", 32, F), ("OF1", 32, F), ("OF2", 32, F), ("OFK", 16, U), ("OFX", 16, U),
+        ("BU", 16, U), ("EXK", NP, F), ("EXB", NP, F), ("KR", NP, U), ("E", 16 * NP, B), ("FD", NP, B), ("FS", NP, F),
+        ("BR", NP, F), ("EG", NP, F), ("ES", NP, F), ("T4", NP, B), ("XG", NP, B), ("XV", NP, B),
+        ("SKF", NP, F), ("SCE", NP, F), ("THO", NP, F), ("RD", NP, B), ("PN", NP, B), ("EA", NP * 2, F),
+        ("RL", 16, F), ("BH", 16, F), ("BH2", 16, F), ("HN", 16, F), ("DW", 16, F), ("DW2", 16, F), ("EJ", 16, F), ("WF", 16, F),
+        ("PJ1", NP, B), ("PJ2", NP, B), ("HI", 16, I), ("HA", 16, I), ("HG", 16, F), ("YF", NP, F), ("YO", NP, F), ("YT", NP, F),
+        ("IC", NP, I), ("IP", 1, I), ("CMI", NP, I), ("ICF", NP, F), ("CMF", NP, F), ("CGF", NP, F),
+        ("PMI", 1, I), ("PAI", 1, I), ("COL", 16, F), ("TG", 4, F), ("TGA", 4, F),
+        ("IDF", 128, F), ("BDF", 128, F), ("YW", 128, F), ("LUS", 512, F), ("WS", 144, F), ("WA", 144, B), ("WB", 144, B), ("WH", 144, B),
+        ("BD17", 128, B), ("W1", 128, B), ("IDB", 128, B), ("NIDB", 128, B), ("DIAG", NP, F), ("RS", NP, F), ("SEG", NP, F),
+        ("PW", 16, F), ("PWD", 16, F), ("POFF", 16, U), ("TH", NP, B), ("THD", NP, F), ("TR", 16, F), ("TRS", 16, F), ("SOFF", NP, U)]:
+    _sb(_n, _w, _d)
+COLS = ["PF", "PM", "PG", "PG15", "PAR", "PA1", "ODD", "EVN", "KCOL", "KEV", "K1", "POW", "WTF"]
+for _n in ["pA0", "pB0", "pA1", "pB1", "pL", "pR", "pR2", "pD"]:
+    _S[_n] = ("psum", [128, 512], F)
+SCRATCH = _S
+NDMA = 24
+SEMAPHORES = (["qV", "qS", "qT", "qG", "loc", "aW", "aF"] + ["aE%d" % t for t in range(NT)] + ["aP%d" % t for t in range(NT)]
+              + ["aH%d" % t for t in range(NT)] + ["d%d" % k for k in range(NDMA)])
+
+
+def rank_program(g, core, T, topo):
+    rank = T.rank_of(core)
+    if rank is None:
+        return
+    nxt, prv = T.cores[(rank + 1) % 4], T.cores[(rank + 3) % 4]
+    op = AluOpType
+    AF = ActivationFunctionType
+    queues = {"V": g.vector, "S": g.scalar, "T": g.tensor, "G": g, "Y": g.sync}
+    count = {}
+    known = {q: {} for q in queues}
+    log = {}
+    order = [0]
+    ndma = [0]
+    nloc = [0]
+
+    def A(n, a=0, b=None, s=1):
+        if n in COLS:
+            return ("COL", COLS.index(n), COLS.index(n) + 1, 1)
+        return (n, a, _S[n][1][1] if b is None else b, s)
+
+    def IND(w, o):
+        return ("ind", w, o)
+
+    def ap(x):
+        if not isinstance(x, tuple):
+            return x
+        if x[0] == "ind":
+            return ap(x[1]).indirect(ap(x[2]))
+        n, a, b, s = x
+        return T[n][:, a:b] if s == 1 else T[n][:, a:b:s]
+
+    def regs(x):
+        if not isinstance(x, tuple):
+            return []
+        return [x[1], x[2]] if x[0] == "ind" else [x]
+
+    def psum(n):
+        return _S[n][0] == "psum"
+
+    def need(q, reads, writes):
+        ev = []
+        for lst, wr in ((reads, False), (writes, True)):
+            for r in lst:
+                for e in log.get(r[0], []):
+                    if psum(r[0]):
+                        if e[3] == q and (q == "T" or not (wr or e[2])):
+                            continue
+                        ev.append(e[4])
+                    elif e[0] < r[2] and r[1] < e[1] and (wr or e[2]):
+                        ev.append(e[4])
+        ev.sort(key=lambda e: -e[0])
+        for e in ev:
+            if known[q].get(e[1], 0) >= e[2]:
+                continue
+            queues[q].wait_ge(T.sem[e[1]], e[2])
+            for k, v in e[3].items():
+                known[q][k] = max(known[q].get(k, 0), v)
+
+    def note(q, reads, writes, event):
+        for r in writes:
+            l = log.setdefault(r[0], [])
+            if r[3] == 1 or psum(r[0]):
+                lo, hi = (0, 1 << 20) if psum(r[0]) and q != "T" else (r[1], r[2])
+                l[:] = [e for e in l if not (lo <= e[0] and e[1] <= hi)]
+            l.append((r[1], r[2], True, q, event))
+        for r in reads:
+            l = log.setdefault(r[0], [])
+            l[:] = [e for e in l if not (not e[2] and e[3] == q and r[1] <= e[0] and e[1] <= r[2])]
+            l.append((r[1], r[2], False, q, event))
+
+    def event(q, sem, val):
+        order[0] += 1
+        c = dict(known[q])
+        c[sem] = val
+        return (order[0], sem, val, c)
+
+    def emit(q, reads, writes, fn):
+        need(q, reads, writes)
+        sem = "q" + q
+        count[sem] = count.get(sem, 0) + 1
+        fn().then_inc(T.sem[sem], 1)
+        note(q, reads, writes, event(q, sem, count[sem]))
+
+    def external(x, sem, val):
+        order[0] += 1
+        log.setdefault(x[0], []).append((x[1], x[2], True, "X", (order[0], sem, val, {sem: val})))
+
+    def tt(out, a, b, o, q="V"):
+        wr = [out[1]] if out[0] == "ind" else [out]
+        rd = regs(a) + regs(b) + ([out[2]] if out[0] == "ind" else [])
+        emit(q, rd, wr, lambda: g.vector.tensor_tensor(ap(out), ap(a), ap(b), o))
+
+    def ts(out, a, s1, o1, s2=None, o2=None):
+        rd = regs(a) + regs(s1) + regs(s2)
+        if o2 is None:
+            emit("V", rd, [out], lambda: g.vector.tensor_scalar(ap(out), ap(a), ap(s1), None, o1))
+        else:
+            emit("V", rd, [out], lambda: g.vector.tensor_scalar(ap(out), ap(a), ap(s1), ap(s2), o1, o2))
+
+    def cp(out, a):
+        wr = [out[1]] if out[0] == "ind" else [out]
+        emit("V", regs(a) + ([out[2]] if out[0] == "ind" else []), wr, lambda: g.vector.tensor_copy(ap(out), ap(a)))
+
+    def scan(out, d0, d1, init, o0, o1):
+        emit("V", [d0, d1], [out], lambda: g.vector.tensor_tensor_scan(ap(out), ap(d0), ap(d1), init, o0, o1))
+
+    def vtr(out, a):
+        emit("V", [a], [out], lambda: g.vector.transpose(ap(out), ap(a)))
+
+    def fill(out, c):
+        emit("V", [], [out], lambda: g.vector.memset(ap(out), c))
+
+    def act(out, a, f, bias=0.0, scale=1.0):
+        emit("S", regs(a) + regs(bias) + regs(scale), [out],
+             lambda: g.scalar.activation(ap(out), ap(a), f, bias=ap(bias), scale=ap(scale)))
+
+    def mm(out, l, r, start, stop):
+        emit("T", [l, r], [out], lambda: g.tensor.matmul(ap(out), ap(l), ap(r), start, stop))
+
+    def dma(q, out, in_, reads, writes):
+        need(q, reads, writes)
+        sem = "d%d" % ndma[0]
+        ndma[0] += 1
+        queues[q].dma_start(out, in_).then_inc(T.sem[sem], 16)
+        note(q, reads, writes, event(q, sem, 16))
+        return sem
+
+    def send(dst, out, in_, sem):
+        need("G", [in_], [])
+        rid, pid = topo.addr(dst)[:2]
+        m = topo.engines(core, dst)[:8]
+        mask = sum(1 << e for e in m)
+        g.remote_dma(ap(out), ap(in_), T.sem[sem], T.sem.loc, pid, rid, mask)
+        nloc[0] += len(m)
+
+    def arrives(src, x, sem):
+        external(x, sem, len(topo.engines(src, core)[:8]))
+
+    for q, n, src in (("Y", "OWN", T.own), ("Y", "WL", T.wall), ("Y", "HI0", T.hold), ("Y", "WTI", T.wt)):
+        dma(q, T[n][:, :], src[:, :], [], [A(n)])
+    dma("S", T.PN[:, :], T.price[:, :], [], [A("PN")])
+    for k in range(4):
+        a, b = 896 * k, 896 * k + 896
+        dma("YS"[k % 2], T.KI[:, a:b], T.kin[:, a:b], [], [A("KI", a, b)])
+    for k in range(2):
+        a, b = 1792 * k, 1792 * k + 1792
+        dma("YS"[k % 2], T.X[:, a:b], T.x[:, a:b], [], [A("X", a, b)])
+
+    emit("G", [], [A("IC")], lambda: g.iota(T.IC[:, :], [[1, NP]], 0, 0))
+    emit("G", [], [A("IP")], lambda: g.iota(T.IP[:, :], [[1, 1]], 0, 1))
+    send(prv, A("WR"), A("WL"), "aW")
+    arrives(nxt, A("WR"), "aW")
+    emit("G", [], [A("H", 0, V)], lambda: g.iota(T.H[:, 0:V], [[1, V]], 0, 0, allow_small_or_imprecise_dtypes=True))
+    ts(A("CMI"), A("IC"), 15, op.bitwise_and)
+    ts(A("PMI"), A("IP"), 15, op.bitwise_and)
+    ts(A("PAI"), A("IP"), 4, op.arith_shift_right, 1, op.bitwise_and)
+    cp(A("SOFF"), A("IC"))
+    cp(A("ICF"), A("IC"))
+    cp(A("PF"), A("IP"))
+    cp(A("CMF"), A("CMI"))
+    cp(A("PM"), A("PMI"))
+    cp(A("PAR"), A("PAI"))
+    cp(A("RE", 0, 16), A("OWN"))
+    ts(A("RP", 0, NP), A("PN"), -1.0, op.mult, 15.0, op.add)
+    tt(A("CGF"), A("ICF"), A("CMF"), op.subtract)
+    tt(A("PG"), A("PF"), A("PM"), op.subtract)
+    ts(A("KCOL"), A("PM"), 4096.0, op.mult)
+    ts(A("DIAG"), A("CMF"), A("PM"), op.is_equal)
+    ts(A("PG15"), A("PG"), 15.0, op.add)
+    ts(A("WS"), A("ICF", 0, 144), A("PG15"), op.is_equal)
+    ts(A("IDF"), A("ICF", 0, 128), A("PF"), op.is_equal)
+    ts(A("WA"), A("WS"), 65536.0, op.mult)
+    ts(A("WB"), A("WS"), -BIG, op.mult)
+    cp(A("RH", 0, 16), A("HI0"))
+    ts(A("RS"), A("CMF"), 0.0, op.is_equal, float(2 ** 25), op.mult)
+
+    def late_constants():
+        ts(A("SEG"), A("CMF"), 0.0, op.not_equal)
+        ts(A("PA1"), A("PAR"), -1.0, op.mult, 1.0, op.add)
+        for u in range(2):
+            for s in range(2):
+                j = 2 * u + s
+                ts(A("TGA", j, j + 1), A("PF"), 16.0 * (s - u) + 1.0, op.add, A("PAR" if u else "PA1"), op.mult)
+                ts(A("TG", j, j + 1), A("TGA", j, j + 1), -1.0, op.add)
+                ts(A("LUS", 128 * j, 128 * j + 128), A("ICF", 0, 128), A("TG", j, j + 1), op.is_equal)
+        ts(A("BDF"), A("CGF", 0, 128), A("PG"), op.is_equal)
+        ts(A("TRS"), A("ICF", 0, 16), 16.0, op.mult, float(V), op.add)
+        ts(A("TR"), A("TRS"), A("PM"), op.add)
+        ts(A("TRS"), A("TR"), 1.0 / 8192, op.mult)
+        for i in range(16):
+            fill(A("PW", i, i + 1), float(2 ** (16 - i)))
+        cp(A("POFF"), A("CMI", 0, 16))
+        ts(A("BD17"), A("BDF"), -float(2 ** 17), op.mult)
+        cp(A("IDB"), A("IDF"))
+        ts(A("NIDB"), A("IDF"), -1.0, op.mult)
+        ts(A("PWD"), A("ICF", 0, 16), 0.0, op.mult, A("PM"), op.add)
+        cp(A("POFF"), A("PWD"))
+        cp(A("TH"), IND(A("PW"), A("POFF")))
+        ts(A("THD"), A("DIAG"), -float(2 ** 17), op.mult, float(2 ** 17), op.add)
+        tt(A("PWD"), A("PW"), A("DIAG", 0, 16), op.mult)
+        emit("V", [A("PWD")], [A("POW")], lambda: g.vector.tensor_reduce(ap(A("POW")), T.PWD[:, :], AxisListType.X, op.add))
+        ts(A("W1"), A("BDF"), A("POW"), op.mult, -0.5, op.mult)
+        ts(A("PAI"), A("PMI"), 1, op.bitwise_and)
+        cp(A("ODD"), A("PAI"))
+        ts(A("EVN"), A("ODD"), -1.0, op.mult, 1.0, op.add)
+        ts(A("KEV"), A("KCOL"), -1.0, op.mult, A("EVN"), op.mult)
+        ts(A("K1"), A("PM"), 1.0, op.add)
+        ts(A("YW"), A("BDF"), A("K1"), op.mult)
+        cp(A("WTF"), A("WTI"))
+        ts(A("WH"), A("WS"), A("WTF"), op.mult)
+
+    late_constants()
+    for k in range(4):
+        a, b = 896 * k, 896 * k + 896
+        cp(A("K", a, b), A("KI", a, b))
+    pend = []
+
+    def pa(c):
+        return ("pA0", "pB0") if c < NCH - 1 else ("pA1", "pB1")
+
+    for t in range(NT):
+        e = A("RE", 16 * t, 16 * t + 16)
+        price = A("RP", NP * t, NP * t + NP)
+        hold = A("RH", 16 * t, 16 * t + 16)
+        jub = t % TERM == TERM - 1
+        last = t == NT - 1
+        if t:
+            arrives(prv, price, "aP%d" % t)
+            arrives(prv, e, "aE%d" % t)
+            arrives(prv, hold, "aH%d" % t)
+        Kg, Xg = A("K", 0, V), A("X", 0, V)
+
+        def rep(c):
+            act(A("PR", 1024 * c, 1024 * c + 1024), IND(price, A("SOFF", CH * c, CH * c + CH)), AF.Identity)
+
+        def part(n, c):
+            w = 1024 if c < NCH - 1 else 512
+            return A(n, int(1024 * c), int(1024 * c) + w)
+
+        def dif(c):
+            x = part("D", c)
+            tt(x, IND(Xg, A("CU", x[1] // 16, x[2] // 16)), part("PR", c), op.add)
+
+        def cmp(c):
+            ts(part("GE", c), part("D", c), 15.0, op.is_ge, -0.53125, op.add)
+
+        def absd(c):
+            act(part("AB", c), part("D", c), AF.Abs, bias=-15.0)
+
+        def sums(c):
+            a, b = pa(c)
+            lo, hi = CH * c, CH * c + CH
+            for k in range(16):
+                mm(A(b, lo, hi), A("WB", 15 - k, 143 - k), A("GE", 1024 * c + k, 1024 * c + 1024, 16), k == 0, k == 15)
+            mm(A(a, lo, hi), A("IDF"), A("KC0", lo, hi), True, False)
+            for k in range(16):
+                mm(A(a, lo, hi), A("WA", 15 - k, 143 - k), A("AB", 1024 * c + k, 1024 * c + 1024, 16), False, k == 15)
+
+        def best(c0, c1):
+            lo, hi = CH * c0, CH * c1
+            a, b = pa(c0)
+            tt(A("KB", lo, hi), A(b, lo, hi), A("KC0", lo, hi), op.max)
+            tt(A("KEY", lo, hi), A(a, lo, hi), A("KB", lo, hi), op.min)
+            vtr(A("T1", lo, hi), A("KEY", lo, hi))
+            scan(A("SC", lo, hi), A("RS", lo, hi), A("T1", lo, hi), float(2 ** 25), op.add, op.min)
+
+        rep(0)
+        rep(1)
+        cp(A("CU"), IND(Kg, e))
+        dif(0)
+        ts(A("KC0"), A("CU"), A("KCOL"), op.add)
+        cmp(0)
+        absd(0)
+        rep(2)
+        sums(0)
+        dif(1)
+        cmp(1)
+        absd(1)
+        rep(3)
+        sums(1)
+        dif(2)
+        cmp(2)
+        absd(2)
+        sums(2)
+        dif(3)
+        absd(3)
+        dif(3.5)
+        cmp(3)
+        absd(3.5)
+        cmp(3.5)
+        sums(3)
+        best(0, NCH - 1)
+        best(NCH - 1, NCH)
+        ts(A("EV"), e, float(V), op.add)
+        ts(A("EF"), e, 1.0 / 8192, op.mult)
+        if t == 0:
+            cp(A("WF"), A("WR"))
+        while pend:
+            pend.pop(0)()
+        tt(A("EMT"), A("EF"), A("TRS"), op.subtract)
+        act(A("T4"), price, AF.Identity, bias=163.375, scale=-0.25)
+        act(A("SCE"), A("KC0"), AF.Identity, bias=A("KEV"), scale=A("EVN"))
+        for u in range(2):
+            for s in range(2):
+                j = 2 * u + s
+                mm(A("pL", u, 16, 2), A("LUS", 128 * j, 128 * j + 128), A("SC", 15 + 16 * s, NP, 32), s == 0, s == 1)
+        mm(A("pD", 0, NP), A("IDB"), A("TH"), True, False)
+        cp(A("MI"), A("pL", 0, 16))
+        ts(A("FB"), A("pL", 0, 16), 65536.0, op.is_ge, 8192.0, op.mult)
+        ts(A("BI"), A("MI"), 4095, op.bitwise_and)
+        tt(A("KT"), A("BI"), A("FB"), op.add)
+        tt(A("KL"), A("KT"), A("EV"), op.min)
+        tt(A("EXK"), IND(A("KL"), A("SOFF", 0, 16)), A("DIAG"), op.mult)
+        mm(A("pR", 0, NP), A("BDF"), A("EXK"), True, True)
+        cp(A("BU"), A("BI"))
+        ts(A("OFF"), A("pL", 0, 16), 65536.0, op.is_lt)
+        tt(A("BMT"), A("BI"), A("TR"), op.subtract)
+        tt(A("WW", 0, 16), A("EMT"), A("FB"), op.mult)
+        tt(A("WW", 16, 32), A("BMT"), A("OFF"), op.mult)
+        act(A("XG"), IND(Xg, A("BU")), AF.Identity)
+        cp(A("KR"), A("pR", 0, NP))
+        ea = 0
+        for j in range(NE, 16):
+            w = NP - 16 * j
+            act(A("EA", ea, ea + w), A("pR", 16 * j, NP), AF.Abs, bias=A("KL", j, j + 1), scale=-1.0)
+            ea += w
+        act(A("E", NP * NE, NP * NE + ea), A("EA", 0, ea), AF.Relu, bias=1.0, scale=-1.0)
+        act(A("THO"), A("pR", 0, NP), AF.Relu, bias=-float(2 ** 17 * (V - 1)), scale=float(2 ** 17))
+        ea = NP * NE
+        for j in range(16):
+            lo = 16 * j
+            if j < NE:
+                x = A("E", NP * j + lo, NP * j + NP)
+                ts(x, A("KR", lo, NP), A("KL", j, j + 1), op.is_equal)
+            else:
+                x = A("E", ea, ea + NP - lo)
+                ea += NP - lo
+            mm(A("pD", lo, lo + 16), A("W1"), A("E", x[1], x[1] + 16), False, j == 15)
+            if j < 15:
+                mm(A("pD", lo + 16, NP), A("BD17"), A("E", x[1] + 16, x[2]), False, False)
+        tt(A("EXB"), IND(A("BI"), A("SOFF", 0, 16)), A("DIAG"), op.mult)
+        mm(A("pR2", 0, NP), A("BDF"), A("EXB"), True, True)
+        act(A("BR"), A("pR2", 0, NP), AF.Identity)
+        mm(A("pB1", 0, NP), A("IDB"), A("XG"), True, False)
+        mm(A("pB1", 0, NP), A("NIDB"), A("T4"), False, True)
+        tt(A("FD"), A("pD", 0, NP), A("THD"), op.is_gt)
+        if RDF:
+            tt(A("RD"), A("pD", 0, NP), A("THO"), op.is_gt)
+        scan(A("FS"), A("SEG"), A("FD"), 0.0, op.mult, op.add)
+        fl = A("FS", 15, NP, 16)
+        tt(A("OF1", 0, 16), fl, A("WW", 0, 16), op.mult)
+        if not RDF:
+            tt(A("RD"), A("pD", 0, NP), A("THO"), op.is_gt)
+        tt(A("OF2", 0, 16), A("OF1", 0, 16), A("TR"), op.add)
+        cp(A("OFK"), A("OF2", 0, 16))
+        pn = A("PN") if jub else A("PO", NP * t, NP * t + NP)
+        mm(A("pA1", 0, NP), A("IDB"), price, True, False)
+        mm(A("pA1", 0, NP), A("NIDB"), A("RD"), False, True)
+        act(pn, A("pA1", 0, NP), AF.Relu)
+        if not jub:
+            send(nxt, A("RP", NP * t + NP, NP * t + 2 * NP), pn, "aP%d" % (t + 1))
+        act(A("SKF"), IND(Kg, A("BU")), AF.Identity, scale=A("ODD"))
+        act(A("XV"), A("pB1", 0, NP), AF.Relu, bias=160.0)
+        if last:
+            ybase(g, T, A, mm, act, AF, range(3, 7))
+            mm(A("pA1", 0, NP), A("YW"), A("SKF"), True, False)
+            mm(A("pA1", 0, NP), A("YW"), A("SCE"), False, True)
+            act(A("YF"), A("pA1", 0, NP), AF.Identity)
+        cp(IND(A("H"), A("OFK")), A("BR"))
+        tt(A("EG"), IND(A("H", 0, V), e), A("DIAG"), op.mult)
+
+        def xpart():
+            tt(A("OF1", 16, 32), fl, A("WW", 16, 32), op.mult)
+            tt(A("OF2", 16, 32), A("OF1", 16, 32), A("TR"), op.add)
+            cp(A("OFX"), A("OF2", 16, 32))
+            cp(IND(A("X"), A("OFX")), A("XV"))
+
+        def hpart(out, hold=hold, fl=fl):
+            tt(A("RL"), fl, A("OFF"), op.mult)
+            tt(A("BH"), A("BI"), hold, op.subtract)
+            tt(A("BH2"), A("RL"), A("BH"), op.mult)
+            tt(out, A("BH2"), hold, op.add)
+
+        def kpart():
+            tt(IND(A("K"), A("OFK")), A("SKF"), A("SCE"), op.add)
+
+        el = A("ES", 15, NP, 16)
+        scan(A("ES"), A("SEG"), A("EG"), 0.0, op.mult, op.add)
+        if not jub:
+            en = A("EN", 16 * t, 16 * t + 16)
+            cp(en, el)
+            send(nxt, A("RE", 16 * t + 16, 16 * t + 32), en, "aE%d" % (t + 1))
+            kpart()
+            xpart()
+
+            def hsend(t=t, hpart=hpart):
+                ho = A("HO", 16 * t, 16 * t + 16)
+                hpart(ho)
+                send(nxt, A("RH", 16 * t + 16, 16 * t + 32), ho, "aH%d" % (t + 1))
+            pend.append(hsend)
+        else:
+            hpart(A("HN"))
+            tt(A("DW"), A("HN"), el, op.subtract)
+            tt(A("DW2"), A("DW"), A("WF"), op.mult)
+            tt(A("EJ"), A("DW2"), el, op.add)
+            en = A("EN", 16 * t, 16 * t + 16)
+            cp(en, A("EJ"))
+            if not last:
+                send(nxt, A("RE", 16 * t + 16, 16 * t + 32), en, "aE%d" % (t + 1))
+            else:
+                cp(A("FO", 0, 16), A("EJ"))
+            xpart()
+            tt(A("PJ1"), IND(Xg, en), A("PN"), op.subtract)
+            ts(A("PJ2"), A("PJ1"), 0.5, op.mult, 167.25, op.add)
+            po = A("PO", NP * t, NP * t + NP)
+            if not last:
+                ts(po, A("PJ2"), -1.0, op.mult, 175.0, op.add)
+            ts(A("PJ1"), A("PJ2"), -160.0, op.add)
+            if not last:
+                send(nxt, A("RP", NP * t + NP, NP * t + 2 * NP), po, "aP%d" % (t + 1))
+                kpart()
+            for j in range(16):
+                mm(A("pL", 0, 16), A("WH", 15 - j, 143 - j), A("PJ1", j, NP, 16), j == 0, j == 15)
+            cp(A("HI"), A("pL", 0, 16))
+
+            def hnew(t=t, ho=A("FO", 16, 32) if last else A("HO", 16 * t, 16 * t + 16)):
+                ts(A("HA"), A("HI"), 4095, op.bitwise_and)
+                ts(A("HG"), A("HA"), float(V), op.is_ge, -float(V), op.mult)
+                tt(ho, A("HA"), A("HG"), op.add)
+                if t < NT - 1:
+                    send(nxt, A("RH", 16 * t + 16, 16 * t + 32), ho, "aH%d" % (t + 1))
+                else:
+                    send(nxt, A("FIN"), A("FO"), "aF")
+            if last:
+                hnew()
+            else:
+                pend.append(hnew)
+        if t == NT - 2:
+            ybase(g, T, A, mm, act, AF, range(0, 3))
+        if last:
+            outs = []
+            outs.append(("Y", dma("Y", T.yh[:, :], T.H[0:128:16, 0:V], [A("H", 0, V)], [])))
+            outs.append(("Y", dma("Y", T.yx[:, :], T.X[:, 0:V], [A("X", 0, V)], [])))
+            cp(IND(A("YK"), A("OFK")), A("YF"))
+            outs.append(("Y", dma("Y", T.yk[:, :], T.YK[0:128:16, 0:V], [A("YK", 0, V)], [])))
+            arrives(prv, A("FIN"), "aF")
+            for k, (x, p, y, o) in enumerate((("EXK", "pR", "YO", T.yo), ("EXB", "pR2", "YT", T.yt))):
+                tt(A(x), IND(A("FIN", 16 * k, 16 * k + 16), A("SOFF", 0, 16)), A("DIAG"), op.mult)
+                mm(A(p, 0, NP), A("BDF"), A(x), True, True)
+                if k:
+                    act(A(y), A(p, 0, NP), AF.Identity)
+                else:
+                    cp(A(y), A(p, 0, NP))
+                outs.append(("YS"[k], dma("YS"[k], o[:, :], T[y][0:128:16, :], [A(y)], [])))
+            for q, s in outs:
+                queues[q].wait_ge(T.sem[s], 16)
+            g.wait_ge(T.sem.loc, nloc[0])
+            for s, n in count.items():
+                g.wait_ge(T.sem[s], n)
+
+
+def ybase(g, T, A, mm, act, AF, blocks):
+    for k in blocks:
+        p = ("pA0", "pB0", "pB1")[k % 3]
+        mm(A(p, 0, 512), A("YW"), A("K", 512 * k, 512 * k + 512), True, True)
+        act(A("YK", 512 * k, 512 * k + 512), A(p, 0, 512), AF.Identity)

@@ -2,7 +2,7 @@ from concourse.bass import DstId, RemoteDMATransfer
 from concourse.mybir import dt, AluOpType, AxisListType, ActivationFunctionType
 
 V, NP, NT, TERM = 3584, 256, 8, 4
-W = V + NP
+W = 2 * V + NP
 CH = 64
 NCH = NP // CH
 RDF = True
@@ -24,20 +24,20 @@ for _n, _w, _d in [
         ("EN", 16 * NT, U), ("PO", NP * NT, B), ("HO", 16 * NT, F), ("FO", 32, F),
         ("CU", NP, U), ("KC0", NP, F), ("PR", 16 * NP, B), ("D", 16 * NP, B), ("AB", 16 * NP, B), ("GE", 16 * NP, B),
         ("KB", NP, F), ("KEY", NP, F), ("T1", NP, F), ("SC", NP, F),
-        ("MI", 16, I), ("BI", 16, I), ("FB", 16, F), ("OFF", 16, F), ("KT", 16, F), ("KL", 16, F), ("EV", 16, F),
-        ("EF", 16, F), ("EMT", 16, F), ("BMT", 16, F), ("WW", 32, F), ("OF1", 32, F), ("OF2", 32, F), ("OFK", 16, U), ("OFX", 16, U),
+        ("MI", 16, I), ("BI", 16, I), ("FB", 16, F), ("KT", 16, F), ("KL", 16, F), ("EV", 16, F),
+        ("KLT", 16, F), ("OF1", 16, F), ("OF2", 16, F), ("OFS", 16, U),
         ("BU", 16, U), ("EXK", NP, F), ("EXB", NP, F), ("KR", NP, U), ("E", 16 * NP, B), ("FD", NP, B), ("FS", NP, F),
         ("BR", NP, F), ("EG", NP, F), ("ES", NP, F), ("T4", NP, B), ("XG", NP, B), ("XV", NP, B),
         ("SKF", NP, F), ("SCE", NP, F), ("THO", NP, F), ("RD", NP, B), ("PN", NP, B), ("EA", NP * 2, F),
         ("RL", 16, F), ("BH", 16, F), ("BH2", 16, F), ("HN", 16, F), ("DW", 16, F), ("DW2", 16, F), ("EJ", 16, F), ("WF", 16, F),
         ("PJ1", NP, B), ("PJ2", NP, B), ("HI", 16, I), ("HA", 16, I), ("HG", 16, F), ("YF", NP, F), ("YO", NP, F), ("YT", NP, F),
-        ("IC", NP, I), ("IP", 1, I), ("CMI", NP, I), ("ICF", NP, F), ("CMF", NP, F), ("CGF", NP, F),
-        ("PMI", 1, I), ("PAI", 1, I), ("COL", 16, F), ("TG", 4, F), ("TGA", 4, F),
+        ("IP", 1, I), ("ICF", NP, F), ("CMF", NP, F), ("CGF", 128, F), ("TRB", 16, F),
+        ("PMI", 1, I), ("PAI", 1, I), ("ODI", 1, I), ("COL", 16, F),
         ("IDF", 128, F), ("BDF", 128, F), ("YW", 128, F), ("LUS", 512, F), ("WS", 144, F), ("WA", 144, B), ("WB", 144, B), ("WH", 144, B),
         ("BD17", 128, B), ("W1", 128, B), ("IDB", 128, B), ("NIDB", 128, B), ("DIAG", NP, F), ("RS", NP, F), ("SEG", NP, F),
-        ("PW", 16, F), ("PWD", 16, F), ("POFF", 16, U), ("TH", NP, B), ("THD", NP, F), ("TR", 16, F), ("TRS", 16, F), ("SOFF", NP, U)]:
+        ("PWD", 16, F), ("TH", NP, B), ("THD", NP, F), ("TR", 16, F), ("SOFF", NP, U)]:
     _sb(_n, _w, _d)
-COLS = ["PF", "PM", "PG", "PG15", "PAR", "PA1", "ODD", "EVN", "KCOL", "KEV", "K1", "POW", "WTF"]
+COLS = ["PF", "PM", "PG", "PG15", "PAR", "PA1", "ODD", "EVN", "KCOL", "KEV", "K1", "POW", "WTF", "PFM", "PFP", "POH"]
 for _n in ["pA0", "pB0", "pA1", "pB1", "pL", "pR", "pR2", "pD"]:
     _S[_n] = ("psum", [128, 512], F)
 SCRATCH = _S
@@ -194,73 +194,68 @@ def rank_program(g, core, T, topo):
         a, b = 1792 * k, 1792 * k + 1792
         dma("YS"[k % 2], T.X[:, a:b], T.x[:, a:b], [], [A("X", a, b)])
 
-    emit("G", [], [A("IC")], lambda: g.iota(T.IC[:, :], [[1, NP]], 0, 0))
-    emit("G", [], [A("IP")], lambda: g.iota(T.IP[:, :], [[1, 1]], 0, 1))
+    def iota(x, pattern, base=0, per=0):
+        flag = {"allow_small_or_imprecise_dtypes": True} if _S[x[0]][2] == F else {}
+        emit("G", [], [x], lambda: g.iota(ap(x), pattern, base, per, **flag))
+
+    iota(A("IP"), [[1, 1]], 0, 1)
+    iota(A("PF"), [[1, 1]], 0, 1)
+    iota(A("CMF"), [[0, 16], [1, 16]])
+    iota(A("ICF"), [[1, NP]])
+    iota(A("CGF"), [[16, 8], [0, 16]])
+    iota(A("TRB"), [[16, 16]], 2 * V)
     send(prv, A("WR"), A("WL"), "aW")
     arrives(nxt, A("WR"), "aW")
-    emit("G", [], [A("H", 0, V)], lambda: g.iota(T.H[:, 0:V], [[1, V]], 0, 0, allow_small_or_imprecise_dtypes=True))
-    ts(A("CMI"), A("IC"), 15, op.bitwise_and)
+    iota(A("H", V, 2 * V), [[1, V]])
     ts(A("PMI"), A("IP"), 15, op.bitwise_and)
     ts(A("PAI"), A("IP"), 4, op.arith_shift_right, 1, op.bitwise_and)
-    cp(A("SOFF"), A("IC"))
-    cp(A("ICF"), A("IC"))
-    cp(A("PF"), A("IP"))
-    cp(A("CMF"), A("CMI"))
+    ts(A("ODI"), A("IP"), 1, op.bitwise_and)
     cp(A("PM"), A("PMI"))
     cp(A("PAR"), A("PAI"))
-    cp(A("RE", 0, 16), A("OWN"))
-    ts(A("RP", 0, NP), A("PN"), -1.0, op.mult, 15.0, op.add)
-    tt(A("CGF"), A("ICF"), A("CMF"), op.subtract)
+    cp(A("ODD"), A("ODI"))
     tt(A("PG"), A("PF"), A("PM"), op.subtract)
+    ts(A("PG15"), A("PG"), 15.0, op.add)
     ts(A("KCOL"), A("PM"), 4096.0, op.mult)
     ts(A("DIAG"), A("CMF"), A("PM"), op.is_equal)
-    ts(A("PG15"), A("PG"), 15.0, op.add)
-    ts(A("WS"), A("ICF", 0, 144), A("PG15"), op.is_equal)
-    ts(A("IDF"), A("ICF", 0, 128), A("PF"), op.is_equal)
-    ts(A("WA"), A("WS"), 65536.0, op.mult)
-    ts(A("WB"), A("WS"), -BIG, op.mult)
-    cp(A("RH", 0, 16), A("HI0"))
     ts(A("RS"), A("CMF"), 0.0, op.is_equal, float(2 ** 25), op.mult)
-
-    def late_constants():
-        ts(A("SEG"), A("CMF"), 0.0, op.not_equal)
-        ts(A("PA1"), A("PAR"), -1.0, op.mult, 1.0, op.add)
-        for u in range(2):
-            for s in range(2):
-                j = 2 * u + s
-                ts(A("TGA", j, j + 1), A("PF"), 16.0 * (s - u) + 1.0, op.add, A("PAR" if u else "PA1"), op.mult)
-                ts(A("TG", j, j + 1), A("TGA", j, j + 1), -1.0, op.add)
-                ts(A("LUS", 128 * j, 128 * j + 128), A("ICF", 0, 128), A("TG", j, j + 1), op.is_equal)
-        ts(A("BDF"), A("CGF", 0, 128), A("PG"), op.is_equal)
-        ts(A("TRS"), A("ICF", 0, 16), 16.0, op.mult, float(V), op.add)
-        ts(A("TR"), A("TRS"), A("PM"), op.add)
-        ts(A("TRS"), A("TR"), 1.0 / 8192, op.mult)
-        for i in range(16):
-            fill(A("PW", i, i + 1), float(2 ** (16 - i)))
-        cp(A("POFF"), A("CMI", 0, 16))
-        ts(A("BD17"), A("BDF"), -float(2 ** 17), op.mult)
-        cp(A("IDB"), A("IDF"))
-        ts(A("NIDB"), A("IDF"), -1.0, op.mult)
-        ts(A("PWD"), A("ICF", 0, 16), 0.0, op.mult, A("PM"), op.add)
-        cp(A("POFF"), A("PWD"))
-        cp(A("TH"), IND(A("PW"), A("POFF")))
-        ts(A("THD"), A("DIAG"), -float(2 ** 17), op.mult, float(2 ** 17), op.add)
-        tt(A("PWD"), A("PW"), A("DIAG", 0, 16), op.mult)
-        emit("V", [A("PWD")], [A("POW")], lambda: g.vector.tensor_reduce(ap(A("POW")), T.PWD[:, :], AxisListType.X, op.add))
-        ts(A("W1"), A("BDF"), A("POW"), op.mult, -0.5, op.mult)
-        ts(A("PAI"), A("PMI"), 1, op.bitwise_and)
-        cp(A("ODD"), A("PAI"))
-        ts(A("EVN"), A("ODD"), -1.0, op.mult, 1.0, op.add)
-        ts(A("KEV"), A("KCOL"), -1.0, op.mult, A("EVN"), op.mult)
-        ts(A("K1"), A("PM"), 1.0, op.add)
-        ts(A("YW"), A("BDF"), A("K1"), op.mult)
-        cp(A("WTF"), A("WTI"))
-        ts(A("WH"), A("WS"), A("WTF"), op.mult)
-
-    late_constants()
+    ts(A("SEG"), A("CMF"), 0.0, op.not_equal)
+    cp(A("SOFF"), A("ICF"))
+    ts(A("WS"), A("ICF", 0, 144), A("PG15"), op.is_equal)
+    act(A("WA"), A("WS"), AF.Identity, scale=65536.0)
+    act(A("WB"), A("WS"), AF.Identity, scale=-BIG)
+    ts(A("RP", 0, NP), A("PN"), -1.0, op.mult, 15.0, op.add)
+    cp(A("RE", 0, 16), A("OWN"))
+    ts(A("IDF"), A("ICF", 0, 128), A("PF"), op.is_equal)
+    act(A("IDB"), A("IDF"), AF.Identity)
+    act(A("NIDB"), A("IDF"), AF.Identity, scale=-1.0)
+    ts(A("BDF"), A("CGF"), A("PG"), op.is_equal)
+    act(A("BD17"), A("BDF"), AF.Identity, scale=-float(2 ** 17))
+    ts(A("PA1"), A("PAR"), -1.0, op.mult, 1.0, op.add)
+    ts(A("PFM"), A("PF"), -16.0, op.add)
+    ts(A("PFP"), A("PF"), 16.0, op.add)
+    for u in range(2):
+        for s in range(2):
+            j = 2 * u + s
+            ts(A("LUS", 128 * j, 128 * j + 128), A("ICF", 0, 128), A(("PFM", "PF", "PFP")[s - u + 1]), op.is_equal, A("PAR" if u else "PA1"), op.mult)
+    ts(A("KB"), A("CMF"), 0.0, op.is_equal, 65536.0, op.mult)
+    ts(A("KEY"), A("SEG"), 0.5, op.mult)
+    scan(A("TH"), A("KEY"), A("KB"), 0.0, op.mult, op.add)
+    act(A("THD"), A("DIAG"), AF.Identity, bias=float(2 ** 17), scale=-float(2 ** 17))
+    tt(A("PWD"), A("TH", 0, 16), A("DIAG", 0, 16), op.mult)
+    emit("V", [A("PWD")], [A("POW")], lambda: g.vector.tensor_reduce(ap(A("POW")), T.PWD[:, :], AxisListType.X, op.add))
+    ts(A("POH"), A("POW"), -0.5, op.mult)
+    act(A("W1"), A("BDF"), AF.Identity, scale=A("POH"))
+    ts(A("TR"), A("TRB"), A("PM"), op.add)
+    ts(A("EVN"), A("ODD"), -1.0, op.mult, 1.0, op.add)
+    ts(A("KEV"), A("KCOL"), -1.0, op.mult, A("EVN"), op.mult)
+    ts(A("K1"), A("PM"), 1.0, op.add)
+    act(A("YW"), A("BDF"), AF.Identity, scale=A("K1"))
+    cp(A("WTF"), A("WTI"))
+    act(A("WH"), A("WS"), AF.Identity, scale=A("WTF"))
+    cp(A("RH", 0, 16), A("HI0"))
     for k in range(4):
         a, b = 896 * k, 896 * k + 896
-        cp(A("K", a, b), A("KI", a, b))
+        cp(A("K", V + a, V + b), A("KI", a, b))
     pend = []
 
     def pa(c):
@@ -276,7 +271,7 @@ def rank_program(g, core, T, topo):
             arrives(prv, price, "aP%d" % t)
             arrives(prv, e, "aE%d" % t)
             arrives(prv, hold, "aH%d" % t)
-        Kg, Xg = A("K", 0, V), A("X", 0, V)
+        Kg, Xg = A("K", V, 2 * V), A("X", 0, V)
 
         def rep(c):
             act(A("PR", 1024 * c, 1024 * c + 1024), IND(price, A("SOFF", CH * c, CH * c + CH)), AF.Identity)
@@ -298,11 +293,13 @@ def rank_program(g, core, T, topo):
         def sums(c):
             a, b = pa(c)
             lo, hi = CH * c, CH * c + CH
+            if c == 0:
+                mm(A("pA0", 0, NP - CH), A("IDF"), A("KC0", 0, NP - CH), True, False)
+                mm(A("pA1", NP - CH, NP), A("IDF"), A("KC0", NP - CH, NP), True, False)
             for k in range(16):
                 mm(A(b, lo, hi), A("WB", 15 - k, 143 - k), A("GE", 1024 * c + k, 1024 * c + 1024, 16), k == 0, k == 15)
-            mm(A(a, lo, hi), A("IDF"), A("KC0", lo, hi), True, False)
             for k in range(16):
-                mm(A(a, lo, hi), A("WA", 15 - k, 143 - k), A("AB", 1024 * c + k, 1024 * c + 1024, 16), False, k == 15)
+                mm(A(a, lo, hi), A("WA", 15 - k, 143 - k), A("AB", 1024 * c + k, 1024 * c + 1024, 16), False, k == 15 and c >= NCH - 2)
 
         def best(c0, c1):
             lo, hi = CH * c0, CH * c1
@@ -340,12 +337,10 @@ def rank_program(g, core, T, topo):
         best(0, NCH - 1)
         best(NCH - 1, NCH)
         ts(A("EV"), e, float(V), op.add)
-        ts(A("EF"), e, 1.0 / 8192, op.mult)
         if t == 0:
             cp(A("WF"), A("WR"))
         while pend:
             pend.pop(0)()
-        tt(A("EMT"), A("EF"), A("TRS"), op.subtract)
         act(A("T4"), price, AF.Identity, bias=163.375, scale=-0.25)
         act(A("SCE"), A("KC0"), AF.Identity, bias=A("KEV"), scale=A("EVN"))
         for u in range(2):
@@ -361,10 +356,7 @@ def rank_program(g, core, T, topo):
         tt(A("EXK"), IND(A("KL"), A("SOFF", 0, 16)), A("DIAG"), op.mult)
         mm(A("pR", 0, NP), A("BDF"), A("EXK"), True, True)
         cp(A("BU"), A("BI"))
-        ts(A("OFF"), A("pL", 0, 16), 65536.0, op.is_lt)
-        tt(A("BMT"), A("BI"), A("TR"), op.subtract)
-        tt(A("WW", 0, 16), A("EMT"), A("FB"), op.mult)
-        tt(A("WW", 16, 32), A("BMT"), A("OFF"), op.mult)
+        tt(A("KLT"), A("KL"), A("TR"), op.subtract)
         act(A("XG"), IND(Xg, A("BU")), AF.Identity)
         cp(A("KR"), A("pR", 0, NP))
         ea = 0
@@ -396,11 +388,11 @@ def rank_program(g, core, T, topo):
             tt(A("RD"), A("pD", 0, NP), A("THO"), op.is_gt)
         scan(A("FS"), A("SEG"), A("FD"), 0.0, op.mult, op.add)
         fl = A("FS", 15, NP, 16)
-        tt(A("OF1", 0, 16), fl, A("WW", 0, 16), op.mult)
+        tt(A("OF1"), fl, A("KLT"), op.mult)
         if not RDF:
             tt(A("RD"), A("pD", 0, NP), A("THO"), op.is_gt)
-        tt(A("OF2", 0, 16), A("OF1", 0, 16), A("TR"), op.add)
-        cp(A("OFK"), A("OF2", 0, 16))
+        tt(A("OF2"), A("OF1"), A("TR"), op.add)
+        cp(A("OFS"), A("OF2"))
         pn = A("PN") if jub else A("PO", NP * t, NP * t + NP)
         mm(A("pA1", 0, NP), A("IDB"), price, True, False)
         mm(A("pA1", 0, NP), A("NIDB"), A("RD"), False, True)
@@ -414,23 +406,20 @@ def rank_program(g, core, T, topo):
             mm(A("pA1", 0, NP), A("YW"), A("SKF"), True, False)
             mm(A("pA1", 0, NP), A("YW"), A("SCE"), False, True)
             act(A("YF"), A("pA1", 0, NP), AF.Identity)
-        cp(IND(A("H"), A("OFK")), A("BR"))
-        tt(A("EG"), IND(A("H", 0, V), e), A("DIAG"), op.mult)
+        cp(IND(A("H"), A("OFS")), A("BR"))
+        tt(A("EG"), IND(A("H", V, 2 * V), e), A("DIAG"), op.mult)
 
         def xpart():
-            tt(A("OF1", 16, 32), fl, A("WW", 16, 32), op.mult)
-            tt(A("OF2", 16, 32), A("OF1", 16, 32), A("TR"), op.add)
-            cp(A("OFX"), A("OF2", 16, 32))
-            cp(IND(A("X"), A("OFX")), A("XV"))
+            cp(IND(A("X"), A("OFS")), A("XV"))
 
-        def hpart(out, hold=hold, fl=fl):
-            tt(A("RL"), fl, A("OFF"), op.mult)
-            tt(A("BH"), A("BI"), hold, op.subtract)
+        def hpart(out, hold=hold):
+            ts(A("RL"), A("OF2"), float(V), op.is_lt)
+            tt(A("BH"), A("OF2"), hold, op.subtract)
             tt(A("BH2"), A("RL"), A("BH"), op.mult)
             tt(out, A("BH2"), hold, op.add)
 
         def kpart():
-            tt(IND(A("K"), A("OFK")), A("SKF"), A("SCE"), op.add)
+            tt(IND(A("K"), A("OFS")), A("SKF"), A("SCE"), op.add)
 
         el = A("ES", 15, NP, 16)
         scan(A("ES"), A("SEG"), A("EG"), 0.0, op.mult, op.add)
@@ -487,10 +476,10 @@ def rank_program(g, core, T, topo):
             ybase(g, T, A, mm, act, AF, range(0, 3))
         if last:
             outs = []
-            outs.append(("Y", dma("Y", T.yh[:, :], T.H[0:128:16, 0:V], [A("H", 0, V)], [])))
+            outs.append(("Y", dma("Y", T.yh[:, :], T.H[0:128:16, V:2 * V], [A("H", V, 2 * V)], [])))
             outs.append(("Y", dma("Y", T.yx[:, :], T.X[:, 0:V], [A("X", 0, V)], [])))
-            cp(IND(A("YK"), A("OFK")), A("YF"))
-            outs.append(("Y", dma("Y", T.yk[:, :], T.YK[0:128:16, 0:V], [A("YK", 0, V)], [])))
+            cp(IND(A("YK"), A("OFS")), A("YF"))
+            outs.append(("Y", dma("Y", T.yk[:, :], T.YK[0:128:16, V:2 * V], [A("YK", V, 2 * V)], [])))
             arrives(prv, A("FIN"), "aF")
             for k, (x, p, y, o) in enumerate((("EXK", "pR", "YO", T.yo), ("EXB", "pR2", "YT", T.yt))):
                 tt(A(x), IND(A("FIN", 16 * k, 16 * k + 16), A("SOFF", 0, 16)), A("DIAG"), op.mult)
@@ -510,5 +499,6 @@ def rank_program(g, core, T, topo):
 def ybase(g, T, A, mm, act, AF, blocks):
     for k in blocks:
         p = ("pA0", "pB0", "pB1")[k % 3]
-        mm(A(p, 0, 512), A("YW"), A("K", 512 * k, 512 * k + 512), True, True)
-        act(A("YK", 512 * k, 512 * k + 512), A(p, 0, 512), AF.Identity)
+        a, b = V + 512 * k, V + 512 * k + 512
+        mm(A(p, 0, 512), A("YW"), A("K", a, b), True, True)
+        act(A("YK", a, b), A(p, 0, 512), AF.Identity)

from concourse.bass import DstId, RemoteDMATransfer
from concourse.mybir import dt, AluOpType, AxisListType, ActivationFunctionType

V, NP, NT, TERM = 3584, 256, 8, 4
W = 2 * V + NP
CH = 64
NCH = NP // CH
RDF = True
NE = 11
BIG = float(2 ** 28)

_S = {}


def _sb(n, w, d):
    _S[n] = ("sbuf", [128, w], d)


F, B, I, U = "float32", "bfloat16", "int32", "uint16"
for _n, _w, _d in [
        ("K", W, F), ("KI", V, I), ("X", W, B), ("H", W, F), ("YK", W, F),
        ("OWN", 16, I), ("WL", 16, I), ("WR", 16, I), ("HI0", 16, I), ("WTI", 1, I),
        ("RE", 16 * NT, U), ("RP", NP * NT, B), ("RH", 16 * NT, F), ("FIN", 32, F),
        ("EN", 16 * NT, U), ("PO", NP * NT, B), ("HO", 16 * NT, F), ("FO", 32, F),
        ("CU", NP, U), ("KC0", NP, F), ("PR", 16 * NP, B), ("D", 16 * NP, B), ("AB", 16 * NP, B), ("GE", 16 * NP, B),
        ("KB", NP, F), ("KEY", NP, F), ("T1", NP, F), ("SC", NP, F),
        ("MI", 16, I), ("BI", 16, I), ("FB", 16, F), ("KT", 16, F), ("KL", 16, F), ("EV", 16, F),
        ("KLT", 16, F), ("OF1", 16, F), ("OF2", 16, F), ("OFS", 16, U),
        ("BU", 16, U), ("EXK", NP, F), ("EXB", NP, F), ("KR", NP, U), ("E", 16 * NP, B), ("FD", NP, B), ("FS", NP, F),
        ("BR", NP, F), ("EG", NP, F), ("ES", NP, F), ("T4", NP, B), ("XG", NP, B), ("XV", NP, B),
        ("SKF", NP, F), ("SCE", NP, F), ("THO", NP, F), ("RD", NP, B), ("PN", NP, B), ("EA", NP * 2, F),
        ("RL", 16, F), ("BH", 16, F), ("BH2", 16, F), ("HN", 16, F), ("DW", 16, F), ("DW2", 16, F), ("EJ", 16, F), ("WF", 16, F),
        ("PJ1", NP, B), ("PJ2", NP, B), ("HI", 16, I), ("HA", 16, I), ("HG", 16, F), ("YF", NP, F), ("YO", NP, F), ("YT", NP, F),
        ("IP", 1, I), ("ICF", NP, F), ("CMF", NP, F), ("CGF", 128, F), ("TRB", 16, F),
        ("PMI", 1, I), ("PAI", 1, I), ("ODI", 1, I), ("COL", 16, F),
        ("IDF", 128, F), ("BDF", 128, F), ("YW", 128, F), ("LUS", 512, F), ("WS", 144, F), ("WA", 144, B), ("WB", 144, B), ("WH", 144, B),
        ("BD17", 128, B), ("W1", 128, B), ("IDB", 128, B), ("NIDB", 128, B), ("DIAG", NP, F), ("RS", NP, F), ("SEG", NP, F),
        ("PWD", 16, F), ("TH", NP, B), ("THD", NP, F), ("TR", 16, F), ("SOFF", NP, U)]:
    _sb(_n, _w, _d)
COLS = ["PF", "PM", "PG", "PG15", "PAR", "PA1", "ODD", "EVN", "KCOL", "KEV", "K1", "POW", "WTF", "PFM", "PFP", "POH"]
for _n in ["pA0", "pB0", "pA1", "pB1", "pL", "pR", "pR2", "pD"]:
    _S[_n] = ("psum", [128, 512], F)
SCRATCH = _S
NDMA = 24
SEMAPHORES = (["qV", "qS", "qT", "qG", "loc", "aW", "aF"] + ["aE%d" % t for t in range(NT)] + ["aP%d" % t for t in range(NT)]
              + ["aH%d" % t for t in range(NT)] + ["d%d" % k for k in range(NDMA)])


def rank_program(g, core, T, topo):
    rank = T.rank_of(core)
    if rank is None:
        return
    nxt, prv = T.cores[(rank + 1) % 4], T.cores[(rank + 3) % 4]
    op = AluOpType
    AF = ActivationFunctionType
    queues = {"V": g.vector, "S": g.scalar, "T": g.tensor, "G": g, "Y": g.sync}
    count = {}
    known = {q: {} for q in queues}
    log = {}
    order = [0]
    ndma = [0]
    nloc = [0]

    def A(n, a=0, b=None, s=1):
        if n in COLS:
            return ("COL", COLS.index(n), COLS.index(n) + 1, 1)
        return (n, a, _S[n][1][1] if b is None else b, s)

    def IND(w, o):
        return ("ind", w, o)

    def ap(x):
        if not isinstance(x, tuple):
            return x
        if x[0] == "ind":
            return ap(x[1]).indirect(ap(x[2]))
        n, a, b, s = x
        return T[n][:, a:b] if s == 1 else T[n][:, a:b:s]

    def regs(x):
        if not isinstance(x, tuple):
            return []
        return [x[1], x[2]] if x[0] == "ind" else [x]

    def psum(n):
        return _S[n][0] == "psum"

    def need(q, reads, writes):
        ev = []
        for lst, wr in ((reads, False), (writes, True)):
            for r in lst:
                for e in log.get(r[0], []):
                    if psum(r[0]):
                        if e[3] == q and (q == "T" or not (wr or e[2])):
                            continue
                        ev.append(e[4])
                    elif e[0] < r[2] and r[1] < e[1] and (wr or e[2]):
                        ev.append(e[4])
        ev.sort(key=lambda e: -e[0])
        for e in ev:
            if known[q].get(e[1], 0) >= e[2]:
                continue
            queues[q].wait_ge(T.sem[e[1]], e[2])
            for k, v in e[3].items():
                known[q][k] = max(known[q].get(k, 0), v)

    def note(q, reads, writes, event):
        for r in writes:
            l = log.setdefault(r[0], [])
            if r[3] == 1 or psum(r[0]):
                lo, hi = (0, 1 << 20) if psum(r[0]) and q != "T" else (r[1], r[2])
                l[:] = [e for e in l if not (lo <= e[0] and e[1] <= hi)]
            l.append((r[1], r[2], True, q, event))
        for r in reads:
            l = log.setdefault(r[0], [])
            l[:] = [e for e in l if not (not e[2] and e[3] == q and r[1] <= e[0] and e[1] <= r[2])]
            l.append((r[1], r[2], False, q, event))

    def event(q, sem, val):
        order[0] += 1
        c = dict(known[q])
        c[sem] = val
        return (order[0], sem, val, c)

    def emit(q, reads, writes, fn):
        need(q, reads, writes)
        sem = "q" + q
        count[sem] = count.get(sem, 0) + 1
        fn().then_inc(T.sem[sem], 1)
        note(q, reads, writes, event(q, sem, count[sem]))

    def external(x, sem, val):
        order[0] += 1
        log.setdefault(x[0], []).append((x[1], x[2], True, "X", (order[0], sem, val, {sem: val})))

    def tt(out, a, b, o, q="V"):
        wr = [out[1]] if out[0] == "ind" else [out]
        rd = regs(a) + regs(b) + ([out[2]] if out[0] == "ind" else [])
        emit(q, rd, wr, lambda: g.vector.tensor_tensor(ap(out), ap(a), ap(b), o))

    def ts(out, a, s1, o1, s2=None, o2=None):
        rd = regs(a) + regs(s1) + regs(s2)
        if o2 is None:
            emit("V", rd, [out], lambda: g.vector.tensor_scalar(ap(out), ap(a), ap(s1), None, o1))
        else:
            emit("V", rd, [out], lambda: g.vector.tensor_scalar(ap(out), ap(a), ap(s1), ap(s2), o1, o2))

    def cp(out, a):
        wr = [out[1]] if out[0] == "ind" else [out]
        emit("V", regs(a) + ([out[2]] if out[0] == "ind" else []), wr, lambda: g.vector.tensor_copy(ap(out), ap(a)))

    def scan(out, d0, d1, init, o0, o1):
        emit("V", [d0, d1], [out], lambda: g.vector.tensor_tensor_scan(ap(out), ap(d0), ap(d1), init, o0, o1))

    def vtr(out, a):
        emit("V", [a], [out], lambda: g.vector.transpose(ap(out), ap(a)))

    def fill(out, c):
        emit("V", [], [out], lambda: g.vector.memset(ap(out), c))

    def act(out, a, f, bias=0.0, scale=1.0):
        emit("S", regs(a) + regs(bias) + regs(scale), [out],
             lambda: g.scalar.activation(ap(out), ap(a), f, bias=ap(bias), scale=ap(scale)))

    def mm(out, l, r, start, stop):
        emit("T", [l, r], [out], lambda: g.tensor.matmul(ap(out), ap(l), ap(r), start, stop))

    def dma(q, out, in_, reads, writes):
        need(q, reads, writes)
        sem = "d%d" % ndma[0]
        ndma[0] += 1
        queues[q].dma_start(out, in_).then_inc(T.sem[sem], 16)
        note(q, reads, writes, event(q, sem, 16))
        return sem

    def send(dst, out, in_, sem):
        need("G", [in_], [])
        rid, pid = topo.addr(dst)[:2]
        m = topo.engines(core, dst)[:8]
        mask = sum(1 << e for e in m)
        g.remote_dma(ap(out), ap(in_), T.sem[sem], T.sem.loc, pid, rid, mask)
        nloc[0] += len(m)

    def arrives(src, x, sem):
        external(x, sem, len(topo.engines(src, core)[:8]))

    for q, n, src in (("Y", "OWN", T.own), ("Y", "WL", T.wall), ("Y", "HI0", T.hold), ("Y", "WTI", T.wt)):
        dma(q, T[n][:, :], src[:, :], [], [A(n)])
    dma("S", T.PN[:, :], T.price[:, :], [], [A("PN")])
    for k in range(4):
        a, b = 896 * k, 896 * k + 896
        dma("YS"[k % 2], T.KI[:, a:b], T.kin[:, a:b], [], [A("KI", a, b)])
    for k in range(2):
        a, b = 1792 * k, 1792 * k + 1792
        dma("YS"[k % 2], T.X[:, a:b], T.x[:, a:b], [], [A("X", a, b)])

    def iota(x, pattern, base=0, per=0):
        flag = {"allow_small_or_imprecise_dtypes": True} if _S[x[0]][2] == F else {}
        emit("G", [], [x], lambda: g.iota(ap(x), pattern, base, per, **flag))

    iota(A("IP"), [[1, 1]], 0, 1)
    iota(A("PF"), [[1, 1]], 0, 1)
    iota(A("CMF"), [[0, 16], [1, 16]])
    iota(A("ICF"), [[1, NP]])
    iota(A("CGF"), [[16, 8], [0, 16]])
    iota(A("TRB"), [[16, 16]], 2 * V)
    send(prv, A("WR"), A("WL"), "aW")
    arrives(nxt, A("WR"), "aW")
    iota(A("H", V, 2 * V), [[1, V]])
    ts(A("PMI"), A("IP"), 15, op.bitwise_and)
    ts(A("PAI"), A("IP"), 4, op.arith_shift_right, 1, op.bitwise_and)
    ts(A("ODI"), A("IP"), 1, op.bitwise_and)
    cp(A("PM"), A("PMI"))
    cp(A("PAR"), A("PAI"))
    cp(A("ODD"), A("ODI"))
    tt(A("PG"), A("PF"), A("PM"), op.subtract)
    ts(A("PG15"), A("PG"), 15.0, op.add)
    ts(A("KCOL"), A("PM"), 4096.0, op.mult)
    ts(A("DIAG"), A("CMF"), A("PM"), op.is_equal)
    ts(A("RS"), A("CMF"), 0.0, op.is_equal, float(2 ** 25), op.mult)
    ts(A("SEG"), A("CMF"), 0.0, op.not_equal)
    cp(A("SOFF"), A("ICF"))
    ts(A("WS"), A("ICF", 0, 144), A("PG15"), op.is_equal)
    act(A("WA"), A("WS"), AF.Identity, scale=65536.0)
    act(A("WB"), A("WS"), AF.Identity, scale=-BIG)
    ts(A("RP", 0, NP), A("PN"), -1.0, op.mult, 15.0, op.add)
    cp(A("RE", 0, 16), A("OWN"))
    ts(A("IDF"), A("ICF", 0, 128), A("PF"), op.is_equal)
    act(A("IDB"), A("IDF"), AF.Identity)
    act(A("NIDB"), A("IDF"), AF.Identity, scale=-1.0)
    ts(A("BDF"), A("CGF"), A("PG"), op.is_equal)
    act(A("BD17"), A("BDF"), AF.Identity, scale=-float(2 ** 17))
    ts(A("PA1"), A("PAR"), -1.0, op.mult, 1.0, op.add)
    ts(A("PFM"), A("PF"), -16.0, op.add)
    ts(A("PFP"), A("PF"), 16.0, op.add)
    for u in range(2):
        for s in range(2):
            j = 2 * u + s
            ts(A("LUS", 128 * j, 128 * j + 128), A("ICF", 0, 128), A(("PFM", "PF", "PFP")[s - u + 1]), op.is_equal, A("PAR" if u else "PA1"), op.mult)
    ts(A("KB"), A("CMF"), 0.0, op.is_equal, 65536.0, op.mult)
    ts(A("KEY"), A("SEG"), 0.5, op.mult)
    scan(A("TH"), A("KEY"), A("KB"), 0.0, op.mult, op.add)
    act(A("THD"), A("DIAG"), AF.Identity, bias=float(2 ** 17), scale=-float(2 ** 17))
    tt(A("PWD"), A("TH", 0, 16), A("DIAG", 0, 16), op.mult)
    emit("V", [A("PWD")], [A("POW")], lambda: g.vector.tensor_reduce(ap(A("POW")), T.PWD[:, :], AxisListType.X, op.add))
    ts(A("POH"), A("POW"), -0.5, op.mult)
    act(A("W1"), A("BDF"), AF.Identity, scale=A("POH"))
    ts(A("TR"), A("TRB"), A("PM"), op.add)
    ts(A("EVN"), A("ODD"), -1.0, op.mult, 1.0, op.add)
    ts(A("KEV"), A("KCOL"), -1.0, op.mult, A("EVN"), op.mult)
    ts(A("K1"), A("PM"), 1.0, op.add)
    act(A("YW"), A("BDF"), AF.Identity, scale=A("K1"))
    cp(A("WTF"), A("WTI"))
    act(A("WH"), A("WS"), AF.Identity, scale=A("WTF"))
    cp(A("RH", 0, 16), A("HI0"))
    for k in range(4):
        a, b = 896 * k, 896 * k + 896
        cp(A("K", V + a, V + b), A("KI", a, b))
    pend = []

    def pa(c):
        return ("pA0", "pB0") if c < NCH - 1 else ("pA1", "pB1")

    for t in range(NT):
        e = A("RE", 16 * t, 16 * t + 16)
        price = A("RP", NP * t, NP * t + NP)
        hold = A("RH", 16 * t, 16 * t + 16)
        jub = t % TERM == TERM - 1
        last = t == NT - 1
        if t:
            arrives(prv, price, "aP%d" % t)
            arrives(prv, e, "aE%d" % t)
            arrives(prv, hold, "aH%d" % t)
        Kg, Xg = A("K", V, 2 * V), A("X", 0, V)

        def rep(c):
            act(A("PR", 1024 * c, 1024 * c + 1024), IND(price, A("SOFF", CH * c, CH * c + CH)), AF.Identity)

        def part(n, c):
            w = 1024 if c < NCH - 1 else 512
            return A(n, int(1024 * c), int(1024 * c) + w)

        def dif(c):
            x = part("D", c)
            tt(x, IND(Xg, A("CU", x[1] // 16, x[2] // 16)), part("PR", c), op.add)

        def cmp(c):
            ts(part("GE", c), part("D", c), 15.0, op.is_ge, -0.53125, op.add)

        def absd(c):
            act(part("AB", c), part("D", c), AF.Abs, bias=-15.0)

        def sums(c):
            a, b = pa(c)
            lo, hi = CH * c, CH * c + CH
            if c == 0:
                mm(A("pA0", 0, NP - CH), A("IDF"), A("KC0", 0, NP - CH), True, False)
                mm(A("pA1", NP - CH, NP), A("IDF"), A("KC0", NP - CH, NP), True, False)
            for k in range(16):
                mm(A(b, lo, hi), A("WB", 15 - k, 143 - k), A("GE", 1024 * c + k, 1024 * c + 1024, 16), k == 0, k == 15)
            for k in range(16):
                mm(A(a, lo, hi), A("WA", 15 - k, 143 - k), A("AB", 1024 * c + k, 1024 * c + 1024, 16), False, k == 15 and c >= NCH - 2)

        def best(c0, c1):
            lo, hi = CH * c0, CH * c1
            a, b = pa(c0)
            tt(A("KB", lo, hi), A(b, lo, hi), A("KC0", lo, hi), op.max)
            tt(A("KEY", lo, hi), A(a, lo, hi), A("KB", lo, hi), op.min)
            vtr(A("T1", lo, hi), A("KEY", lo, hi))
            scan(A("SC", lo, hi), A("RS", lo, hi), A("T1", lo, hi), float(2 ** 25), op.add, op.min)

        rep(0)
        rep(1)
        cp(A("CU"), IND(Kg, e))
        dif(0)
        ts(A("KC0"), A("CU"), A("KCOL"), op.add)
        cmp(0)
        absd(0)
        rep(2)
        sums(0)
        dif(1)
        cmp(1)
        absd(1)
        rep(3)
        sums(1)
        dif(2)
        cmp(2)
        absd(2)
        sums(2)
        dif(3)
        absd(3)
        dif(3.5)
        cmp(3)
        absd(3.5)
        cmp(3.5)
        sums(3)
        best(0, NCH - 1)
        best(NCH - 1, NCH)
        ts(A("EV"), e, float(V), op.add)
        if t == 0:
            cp(A("WF"), A("WR"))
        while pend:
            pend.pop(0)()
        act(A("T4"), price, AF.Identity, bias=163.375, scale=-0.25)
        act(A("SCE"), A("KC0"), AF.Identity, bias=A("KEV"), scale=A("EVN"))
        for u in range(2):
            for s in range(2):
                j = 2 * u + s
                mm(A("pL", u, 16, 2), A("LUS", 128 * j, 128 * j + 128), A("SC", 15 + 16 * s, NP, 32), s == 0, s == 1)
        mm(A("pD", 0, NP), A("IDB"), A("TH"), True, False)
        cp(A("MI"), A("pL", 0, 16))
        ts(A("FB"), A("pL", 0, 16), 65536.0, op.is_ge, 8192.0, op.mult)
        ts(A("BI"), A("MI"), 4095, op.bitwise_and)
        tt(A("KT"), A("BI"), A("FB"), op.add)
        tt(A("KL"), A("KT"), A("EV"), op.min)
        tt(A("EXK"), IND(A("KL"), A("SOFF", 0, 16)), A("DIAG"), op.mult)
        mm(A("pR", 0, NP), A("BDF"), A("EXK"), True, True)
        cp(A("BU"), A("BI"))
        tt(A("KLT"), A("KL"), A("TR"), op.subtract)
        act(A("XG"), IND(Xg, A("BU")), AF.Identity)
        cp(A("KR"), A("pR", 0, NP))
        ea = 0
        for j in range(NE, 16):
            w = NP - 16 * j
            act(A("EA", ea, ea + w), A("pR", 16 * j, NP), AF.Abs, bias=A("KL", j, j + 1), scale=-1.0)
            ea += w
        act(A("E", NP * NE, NP * NE + ea), A("EA", 0, ea), AF.Relu, bias=1.0, scale=-1.0)
        act(A("THO"), A("pR", 0, NP), AF.Relu, bias=-float(2 ** 17 * (V - 1)), scale=float(2 ** 17))
        ea = NP * NE
        for j in range(16):
            lo = 16 * j
            if j < NE:
                x = A("E", NP * j + lo, NP * j + NP)
                ts(x, A("KR", lo, NP), A("KL", j, j + 1), op.is_equal)
            else:
                x = A("E", ea, ea + NP - lo)
                ea += NP - lo
            mm(A("pD", lo, lo + 16), A("W1"), A("E", x[1], x[1] + 16), False, j == 15)
            if j < 15:
                mm(A("pD", lo + 16, NP), A("BD17"), A("E", x[1] + 16, x[2]), False, False)
        tt(A("EXB"), IND(A("BI"), A("SOFF", 0, 16)), A("DIAG"), op.mult)
        mm(A("pR2", 0, NP), A("BDF"), A("EXB"), True, True)
        act(A("BR"), A("pR2", 0, NP), AF.Identity)
        mm(A("pB1", 0, NP), A("IDB"), A("XG"), True, False)
        mm(A("pB1", 0, NP), A("NIDB"), A("T4"), False, True)
        tt(A("FD"), A("pD", 0, NP), A("THD"), op.is_gt)
        if RDF:
            tt(A("RD"), A("pD", 0, NP), A("THO"), op.is_gt)
        scan(A("FS"), A("SEG"), A("FD"), 0.0, op.mult, op.add)
        fl = A("FS", 15, NP, 16)
        tt(A("OF1"), fl, A("KLT"), op.mult)
        if not RDF:
            tt(A("RD"), A("pD", 0, NP), A("THO"), op.is_gt)
        tt(A("OF2"), A("OF1"), A("TR"), op.add)
        cp(A("OFS"), A("OF2"))
        pn = A("PN") if jub else A("PO", NP * t, NP * t + NP)
        mm(A("pA1", 0, NP), A("IDB"), price, True, False)
        mm(A("pA1", 0, NP), A("NIDB"), A("RD"), False, True)
        act(pn, A("pA1", 0, NP), AF.Relu)
        if not jub:
            send(nxt, A("RP", NP * t + NP, NP * t + 2 * NP), pn, "aP%d" % (t + 1))
        act(A("SKF"), IND(Kg, A("BU")), AF.Identity, scale=A("ODD"))
        act(A("XV"), A("pB1", 0, NP), AF.Relu, bias=160.0)
        if last:
            ybase(g, T, A, mm, act, AF, range(3, 7))
            mm(A("pA1", 0, NP), A("YW"), A("SKF"), True, False)
            mm(A("pA1", 0, NP), A("YW"), A("SCE"), False, True)
            act(A("YF"), A("pA1", 0, NP), AF.Identity)
        cp(IND(A("H"), A("OFS")), A("BR"))
        tt(A("EG"), IND(A("H", V, 2 * V), e), A("DIAG"), op.mult)

        def xpart():
            cp(IND(A("X"), A("OFS")), A("XV"))

        def hpart(out, hold=hold):
            ts(A("RL"), A("OF2"), float(V), op.is_lt)
            tt(A("BH"), A("OF2"), hold, op.subtract)
            tt(A("BH2"), A("RL"), A("BH"), op.mult)
            tt(out, A("BH2"), hold, op.add)

        def kpart():
            tt(IND(A("K"), A("OFS")), A("SKF"), A("SCE"), op.add)

        el = A("ES", 15, NP, 16)
        scan(A("ES"), A("SEG"), A("EG"), 0.0, op.mult, op.add)
        if not jub:
            en = A("EN", 16 * t, 16 * t + 16)
            cp(en, el)
            send(nxt, A("RE", 16 * t + 16, 16 * t + 32), en, "aE%d" % (t + 1))
            kpart()
            xpart()

            def hsend(t=t, hpart=hpart):
                ho = A("HO", 16 * t, 16 * t + 16)
                hpart(ho)
                send(nxt, A("RH", 16 * t + 16, 16 * t + 32), ho, "aH%d" % (t + 1))
            pend.append(hsend)
        else:
            hpart(A("HN"))
            tt(A("DW"), A("HN"), el, op.subtract)
            tt(A("DW2"), A("DW"), A("WF"), op.mult)
            tt(A("EJ"), A("DW2"), el, op.add)
            en = A("EN", 16 * t, 16 * t + 16)
            cp(en, A("EJ"))
            if not last:
                send(nxt, A("RE", 16 * t + 16, 16 * t + 32), en, "aE%d" % (t + 1))
            else:
                cp(A("FO", 0, 16), A("EJ"))
            xpart()
            tt(A("PJ1"), IND(Xg, en), A("PN"), op.subtract)
            ts(A("PJ2"), A("PJ1"), 0.5, op.mult, 167.25, op.add)
            po = A("PO", NP * t, NP * t + NP)
            if not last:
                ts(po, A("PJ2"), -1.0, op.mult, 175.0, op.add)
            ts(A("PJ1"), A("PJ2"), -160.0, op.add)
            if not last:
                send(nxt, A("RP", NP * t + NP, NP * t + 2 * NP), po, "aP%d" % (t + 1))
                kpart()
            for j in range(16):
                mm(A("pL", 0, 16), A("WH", 15 - j, 143 - j), A("PJ1", j, NP, 16), j == 0, j == 15)
            cp(A("HI"), A("pL", 0, 16))

            def hnew(t=t, ho=A("FO", 16, 32) if last else A("HO", 16 * t, 16 * t + 16)):
                ts(A("HA"), A("HI"), 4095, op.bitwise_and)
                ts(A("HG"), A("HA"), float(V), op.is_ge, -float(V), op.mult)
                tt(ho, A("HA"), A("HG"), op.add)
                if t < NT - 1:
                    send(nxt, A("RH", 16 * t + 16, 16 * t + 32), ho, "aH%d" % (t + 1))
                else:
                    send(nxt, A("FIN"), A("FO"), "aF")
            if last:
                hnew()
            else:
                pend.append(hnew)
        if t == NT - 2:
            ybase(g, T, A, mm, act, AF, range(0, 3))
        if last:
            outs = []
            outs.append(("Y", dma("Y", T.yh[:, :], T.H[0:128:16, V:2 * V], [A("H", V, 2 * V)], [])))
            outs.append(("Y", dma("Y", T.yx[:, :], T.X[:, 0:V], [A("X", 0, V)], [])))
            cp(IND(A("YK"), A("OFS")), A("YF"))
            outs.append(("Y", dma("Y", T.yk[:, :], T.YK[0:128:16, V:2 * V], [A("YK", V, 2 * V)], [])))
            arrives(prv, A("FIN"), "aF")
            for k, (x, p, y, o) in enumerate((("EXK", "pR", "YO", T.yo), ("EXB", "pR2", "YT", T.yt))):
                tt(A(x), IND(A("FIN", 16 * k, 16 * k + 16), A("SOFF", 0, 16)), A("DIAG"), op.mult)
                mm(A(p, 0, NP), A("BDF"), A(x), True, True)
                if k:
                    act(A(y), A(p, 0, NP), AF.Identity)
                else:
                    cp(A(y), A(p, 0, NP))
                outs.append(("YS"[k], dma("YS"[k], o[:, :], T[y][0:128:16, :], [A(y)], [])))
            for q, s in outs:
                queues[q].wait_ge(T.sem[s], 16)
            g.wait_ge(T.sem.loc, nloc[0])
            for s, n in count.items():
                g.wait_ge(T.sem[s], n)


def ybase(g, T, A, mm, act, AF, blocks):
    for k in blocks:
        p = ("pA0", "pB0", "pB1")[k % 3]
        a, b = V + 512 * k, V + 512 * k + 512
        mm(A(p, 0, 512), A("YW"), A("K", a, b), True, True)
        act(A("YK", a, b), A(p, 0, 512), AF.Identity)
